import numpy as np
import ml_dtypes


def mxq(x, axis, fmt="e4m3"):
    dtype, down = {"e4m3": (ml_dtypes.float8_e4m3fn, 7), "e5m2": (ml_dtypes.float8_e5m2, 14)}[fmt]
    v = np.moveaxis(np.asarray(x, np.float32).astype(ml_dtypes.bfloat16).astype(np.float64), axis, -1)
    blocks = v.reshape(v.shape[:-1] + (-1, 32))
    amax = np.abs(blocks).max(-1, keepdims=True)
    byte = np.maximum(np.where(amax > 0, np.frexp(amax)[1] - 1 + 127, 0) - down, 1)
    scale = np.exp2(byte - 127.0)
    codes = (blocks / scale).astype(np.float32).astype(dtype).astype(np.float64)
    return np.moveaxis((codes * scale).reshape(v.shape), -1, axis)


WIDE = False


def mx_kscale(k):
    if not WIDE:
        return np.ones(k)
    levels = np.array([10, -10, 5, -5, 0])
    if k % 512:
        return np.exp2(np.random.permutation(np.resize(levels, k // 32))).repeat(32)
    a = np.empty((k // 512, 16))
    for p in range(k // 512):
        a[p, :8] = np.random.permutation(np.resize(levels, 8))
        for g in range(8):
            far = levels[np.abs(levels - a[p, g]) >= 10]
            a[p, g + 8] = far[np.random.randint(len(far))]
    return np.exp2(a.ravel()).repeat(32)


def f64(x):
    return np.asarray(x).astype(np.float64)


def striped(idx):
    return np.tile(idx.reshape(-1, 16).T, (8, 1)).astype(np.uint16)


def unstriped(offs):
    return offs[:16].T.reshape(-1).astype(np.int64)


def pack_weight(w):
    k, n = w.shape
    w = f64(np.asarray(w, np.float32).astype(ml_dtypes.bfloat16)).reshape(k // 32, 32, n)
    amax = np.abs(w).max(1)
    byte = np.clip(np.where(amax > 0, np.frexp(amax)[1] - 1 + 127 - 7, 1), 1, 254)
    scaled = (w * np.exp2(127.0 - byte)[:, None, :]).reshape(k, n).astype(np.float32)
    words = np.ascontiguousarray(scaled.reshape(k // 512, 128, 4, n).transpose(0, 1, 3, 2)).astype(ml_dtypes.float8_e4m3fn).view(np.uint8)
    return words, np.ascontiguousarray(byte.astype(np.uint8).reshape(k // 512, 16, n))


def unpack_weight(words, scales):
    g, p, n, _ = words.shape
    vals = np.ascontiguousarray(words).view(ml_dtypes.float8_e4m3fn).astype(np.float64) * np.repeat(np.exp2(scales.astype(np.float64) - 127.0), 8, axis=1)[..., None]
    return vals.transpose(0, 1, 3, 2).reshape(g * 512, n)


K, T, S, D, N, H, V, U = 512, 4096, 1024, 4, 256, 512, 256, 512


def setup_inputs():
    n = np.random.standard_normal
    s = mx_kscale(K)[:, None]
    u = mx_kscale(H)
    packed_xT = pack_weight(n((K, T)) * s)
    return {
        "x_words": packed_xT[0],
        "x_scales": packed_xT[1],
        "hT": (n((K, H)) / np.sqrt(K) / s).astype(np.float32),
        "unit": (np.random.uniform(0.6, 1.4, (H, 1)) * u[:, None]).astype(np.float32),
        "w1": (n((H, N)) / np.sqrt(H) / u[:, None]).astype(np.float32),
        "offs": striped(np.random.permutation(T)[:S]),
        "use": striped(np.random.permutation(np.concatenate([np.arange(V), np.random.randint(0, V, U - V)]))),
    }


def reference(x_words, x_scales, hT, unit, w1, offs, use):
    hTq = mxq(f64(hT), 0, "e4m3")
    xq = unpack_weight(x_words, x_scales)[:, unstriped(offs)]
    y = hTq.T @ xq
    prtop = y.reshape(len(y), -1, D).max(axis=2)
    prexp = np.exp(y - np.repeat(prtop, D, axis=1))
    prsum = prexp.reshape(len(prexp), -1, D).sum(axis=2)
    pr = prexp / np.repeat(prsum, D, axis=1)
    py = pr * y
    ev = py.reshape(len(py), -1, D).sum(axis=2)
    eu = ev[:, unstriped(use)]
    p2 = (pr) ** 2
    conc = p2.reshape(len(p2), -1, D).sum(axis=2)
    cu = conc[:, unstriped(use)]
    hid = f64(unit) * (eu * cu)
    return mxq(f64(w1), 0, "e4m3").T @ mxq(hid, 0, "e4m3")

@@ -1,0 +1,245 @@
+from contextlib import ExitStack
+
+import concourse.mybir as mybir
+from concourse.masks import make_identity
+
+K, T, S, D, N, H, V, U = 512, 4096, 1024, 4, 256, 512, 256, 512
+FLOPS = 2 * K * H * S + 2 * H * N * U
+
+F32 = mybir.dt.float32
+BF16 = mybir.dt.bfloat16
+I32 = mybir.dt.int32
+U32 = mybir.dt.uint32
+U16 = mybir.dt.uint16
+U8 = mybir.dt.uint8
+FP8X4 = mybir.dt.float8_e4m3fn_x4
+ALU = mybir.AluOpType
+ACT = mybir.ActivationFunctionType
+AX = mybir.AxisListType
+
+P = 128
+PACK = 4
+VB = V // P
+HALF = U // 2
+EARLY = 2
+HELD_FROM = 4
+
+
+def tile_picked_ycavqe_conc_p_kernel(tc, x_words, x_scales, hT, unit, w1, offs, use, out):
+    nc = tc.nc
+    with ExitStack() as ctx:
+        keep = ctx.enter_context(tc.tile_pool(name="keep", bufs=1))
+        work = ctx.enter_context(tc.tile_pool(name="work", bufs=3))
+        py = ctx.enter_context(tc.psum_pool(name="py", bufs=4))
+        ps = ctx.enter_context(tc.psum_pool(name="ps", bufs=1))
+
+        offs_sb = keep.tile([P, S // 16], U16, name="offs_sb")
+        use_sb = keep.tile([P, U // 16], U16, name="use_sb")
+        table_words = keep.tile([P, T], I32, name="table_words")
+        table_scales = keep.tile([P, T], U8, name="table_scales")
+        h_raw = [keep.tile([P, PACK, H // 2], F32, name="h_raw%d" % a) for a in range(2)]
+        w_raw = keep.tile([P, PACK, N], F32, name="w_raw")
+        unit_sb = keep.tile([P, PACK], F32, name="unit_sb")
+        ident = keep.tile([P, P], F32, name="ident")
+
+        nc.vector.memset(table_scales[:].bitcast(I32), 0)
+        nc.sync.dma_start(offs_sb[:], offs)
+        words_view = x_words[0].rearrange("p n t -> p (n t)").bitcast(I32)
+        nc.sync.dma_start(table_words[:, : T // 4], words_view[:, : T // 4])
+        for q in range(4):
+            nc.sync.dma_start(
+                table_scales[32 * q : 32 * q + 4, :].bitcast(I32), x_scales[0, 4 * q : 4 * q + 4, :].bitcast(I32)
+            )
+        nc.sync.dma_start(table_words[:, T // 4 :], words_view[:, T // 4 :])
+        h_view = hT.rearrange("(p j) c -> p j c", j=PACK)
+        for a in range(2):
+            nc.sync.dma_start(h_raw[a][:], h_view[:, :, a * (H // 2) : (a + 1) * (H // 2)])
+        nc.sync.dma_start(w_raw[:], w1.rearrange("(p j) n -> p j n", j=PACK))
+        nc.sync.dma_start(use_sb[:], use)
+        nc.sync.dma_start(unit_sb[:], unit.rearrange("(p t) o -> p (t o)", t=PACK))
+        make_identity(nc, ident[:])
+
+        picked_scales = keep.tile([P, S], U8, name="picked_scales")
+        x_sc = keep.tile([P, VB, D, P], U8, name="x_sc", align_bytes=64)
+        nc.vector.tensor_copy(picked_scales[:], table_scales[:].indirect(offs_sb[:]))
+        nc.vector.tensor_copy(x_sc[:], picked_scales[:].rearrange("p (b v d) -> p b d v", b=VB, d=D))
+
+        h_bf = keep.tile([P, PACK, P, PACK], BF16, name="h_bf", align_bytes=64)
+        h_codes = [keep.tile([P, P], U32, name="h_codes%d" % t, align_bytes=64) for t in range(PACK)]
+        h_sc = [keep.tile([P, P], U8, name="h_sc%d" % t, align_bytes=64) for t in range(PACK)]
+        picked_words = [keep.tile([P, P * D], U32, name="picked_words%d" % b) for b in range(VB)]
+        x_codes = [keep.tile([P, D, P], U32, name="x_codes%d" % b, align_bytes=64) for b in range(VB)]
+
+        def pick(b):
+            cols = P * D // 16
+            nc.vector.tensor_copy(
+                picked_words[b][:], table_words[:].bitcast(U32).indirect(offs_sb[:, b * cols : (b + 1) * cols])
+            )
+
+        def deal(b):
+            nc.vector.tensor_copy(x_codes[b][:], picked_words[b][:].rearrange("p (v d) -> p d v", d=D))
+
+        def cast_views(a):
+            m = slice(a * (P // 2), (a + 1) * (P // 2))
+            return (
+                h_bf[:, :, m, :].rearrange("p t m j -> p m t j"),
+                h_raw[a][:].rearrange("p j (m t) -> p m t j", t=PACK),
+            )
+
+        def quant_h(t):
+            nc.vector.quantize_mx(h_codes[t][:].bitcast(FP8X4), h_sc[t][:], h_bf[:, t].rearrange("p m j -> p (m j)"))
+
+        pick(0)
+        nc.scalar.copy(*cast_views(0))
+        deal(0)
+        pick(1)
+        nc.vector.tensor_copy(*cast_views(1))
+        quant_h(0)
+        deal(1)
+        for t in range(1, PACK):
+            quant_h(t)
+
+        w_bf = keep.tile([P, N, PACK], BF16, name="w_bf", align_bytes=64)
+        w_codes = keep.tile([P, N], U32, name="w_codes", align_bytes=64)
+        w_sc = keep.tile([P, N], U8, name="w_sc", align_bytes=64)
+
+        hid_planes = [keep.tile([P, PACK, HALF], BF16, name="hid_planes%d" % r) for r in range(2)]
+
+        order = [(t, b) for t in range(PACK) for b in range(VB)]
+        last = len(order) - 1
+        sum_e = [ps.tile([P, PACK, P], F32, name="sum_e%d" % b) for b in range(VB)]
+        sum_ee = [ps.tile([P, 2, V], F32, name="sum_ee%d" % g) for g in range(2)]
+        log_sum = keep.tile([P, VB, D * P], F32, name="log_sum")
+        y_src = {}
+        e_all = [keep.tile([P, D, P], F32, name="e%d" % n) for n in range(len(order))]
+        ey_all = [keep.tile([P, D, P], F32, name="ey%d" % n) for n in range(len(order))]
+
+        def scores(n):
+            t, b = order[n]
+            y = py.tile([P, D, P], F32, name="y")
+            for d in range(D):
+                nc.tensor.matmul_mx(
+                    y[:, d, :],
+                    lhsT=x_codes[b][:, d, :].bitcast(FP8X4),
+                    lhsT_scale=x_sc[:, b, d, :],
+                    rhs=h_codes[t][:].bitcast(FP8X4),
+                    rhs_scale=h_sc[t][:],
+                    start=True,
+                    stop=True,
+                )
+            y_src[n] = y
+
+        def softmax_terms(n):
+            y = y_src[n]
+            top = work.tile([P, P], F32, name="top")
+            if n >= last - 1:
+                z = log_sum[:, last - n, :].rearrange("p (d i) -> p d i", d=D)
+            else:
+                z_tile = work.tile([P, D, P], F32, name="z_tile")
+                z = z_tile[:]
+            nc.vector.tensor_reduce(top[:], y[:].rearrange("p d i -> p i d"), AX.X, ALU.max)
+            nc.vector.tensor_tensor(z, y[:], top[:].unsqueeze(1).to_broadcast([P, D, P]), ALU.subtract)
+            nc.scalar.activation(e_all[n][:], z, ACT.Exp)
+            if EARLY <= n < HELD_FROM:
+                y_sb = keep.tile([P, D, P], F32, name="y_sb%d" % n)
+                nc.scalar.copy(y_sb[:], y[:])
+                y_src[n] = y_sb
+
+        def add_up(dst, src):
+            for d in range(D):
+                nc.tensor.matmul(dst, lhsT=src[:, d, :], rhs=ident[:], start=d == 0, stop=d == D - 1, is_transpose=True)
+
+        def weigh(n):
+            nc.vector.tensor_tensor(ey_all[n][:], y_src[n][:], e_all[n][:], ALU.mult)
+
+        def sums(n):
+            t, b = order[n]
+            if n < EARLY:
+                weigh(n)
+            ee = work.tile([P, D, P], F32, name="ee")
+            nc.scalar.activation(ee[:], e_all[n][:], ACT.Square)
+            add_up(sum_e[b][:, t, :], e_all[n])
+            add_up(sum_ee[t // 2][:, t % 2, b * P : (b + 1) * P], ee)
+
+        for n in range(HELD_FROM):
+            scores(n)
+        softmax_terms(0)
+        for n in range(len(order)):
+            if n + 1 < len(order):
+                softmax_terms(n + 1)
+            sums(n)
+            if n + HELD_FROM < len(order):
+                scores(n + HELD_FROM)
+
+        for b in range(VB):
+            nc.scalar.activation(log_sum[:, b, :], sum_e[b][:].rearrange("p t v -> p (t v)"), ACT.Ln)
+
+        for n in (4, 5, 2, 3, 6, 7):
+            weigh(n)
+        sum_ey = [py.tile([P, D, P], F32, name="y") for g in range(2)]
+        for n in (0, 1, 4, 5, 2, 3, 6, 7):
+            t, b = order[n]
+            add_up(sum_ey[t // 2][:, 2 * (t % 2) + b, :], ey_all[n])
+        nc.vector.tensor_copy(
+            w_bf[:].rearrange("p (c i) j -> p c j i", i=4), w_raw[:].rearrange("p j (c i) -> p c j i", i=4)
+        )
+        nc.vector.quantize_mx(w_codes[:].bitcast(FP8X4), w_sc[:], w_bf[:].rearrange("p n j -> p (n j)"))
+
+        windows = [keep.tile([P, 2 * V], F32, name="window%d" % t) for t in range(PACK)]
+        inv3 = [keep.tile([P, VB, P], F32, name="inv3_%d" % t) for t in range(PACK)]
+        for t in range(PACK):
+            nc.scalar.activation(inv3[t][:], log_sum[:, :, t * P : (t + 1) * P], ACT.Exp, scale=-3.0)
+
+        def scaled(t):
+            nc.vector.scalar_tensor_tensor(
+                windows[t][:, V:],
+                sum_ey[t // 2][:, 2 * (t % 2) : 2 * (t % 2) + 2, :].rearrange("p b v -> p (b v)"),
+                unit_sb[:, t : t + 1],
+                inv3[t][:].rearrange("p b v -> p (b v)"),
+                ALU.mult,
+                ALU.mult,
+            )
+
+        def finish(t):
+            nc.vector.tensor_tensor(windows[t][:, :V], sum_ee[t // 2][:, t % 2, :], windows[t][:, V:], ALU.mult)
+
+        def fetch(t, r):
+            cols = HALF // 16
+            src = windows[t][:].indirect(use_sb[:, r * cols : (r + 1) * cols])
+            if r == 0 and t >= 2:
+                nc.vector.tensor_copy(hid_planes[r][:, t, :], src)
+            else:
+                nc.scalar.activation(hid_planes[r][:, t, :], src, ACT.Copy)
+
+        scaled(0)
+        for t in range(PACK):
+            if t + 1 < PACK:
+                scaled(t + 1)
+            finish(t)
+        for r in range(2):
+            for t in range(PACK):
+                fetch(t, r)
+
+        for r in range(2):
+            hid_bf = keep.tile([P, HALF, PACK], BF16, name="hid_bf%d" % r, align_bytes=64)
+            hid_codes = keep.tile([P, HALF], U32, name="hid_codes%d" % r, align_bytes=64)
+            hid_sc = keep.tile([P, HALF], U8, name="hid_sc%d" % r, align_bytes=64)
+            nc.vector.tensor_copy(
+                hid_bf[:].rearrange("p (c i) t -> p c t i", i=4), hid_planes[r][:].rearrange("p t (c i) -> p c t i", i=4)
+            )
+            nc.vector.quantize_mx(hid_codes[:].bitcast(FP8X4), hid_sc[:], hid_bf[:].rearrange("p r t -> p (r t)"))
+            for mt in range(N // P):
+                acc = py.tile([P, D, P], F32, name="y")
+                acc_cols = acc[:].rearrange("p d i -> p (d i)")[:, :HALF]
+                nc.tensor.matmul_mx(
+                    acc_cols,
+                    lhsT=w_codes[:, mt * P : (mt + 1) * P].bitcast(FP8X4),
+                    lhsT_scale=w_sc[:, mt * P : (mt + 1) * P],
+                    rhs=hid_codes[:].bitcast(FP8X4),
+                    rhs_scale=hid_sc[:],
+                    start=True,
+                    stop=True,
+                )
+                res = keep.tile([P, HALF], F32, name="res%d_%d" % (r, mt))
+                nc.scalar.copy(res[:], acc_cols)
+                nc.sync.dma_start(out[mt * P : (mt + 1) * P, r * HALF : (r + 1) * HALF], res[:])

@@ -21,7 +21,6 @@ P = 128
 PACK = 4
 VB = V // P
 HALF = U // 2
-EARLY = 2
 HELD_FROM = 4
 
 
@@ -65,8 +64,8 @@ def tile_picked_ycavqe_conc_p_kernel(tc, x_words, x_scales, hT, unit, w1, offs, 
         nc.vector.tensor_copy(x_sc[:], picked_scales[:].rearrange("p (b v d) -> p b d v", b=VB, d=D))
 
         h_bf = keep.tile([P, PACK, P, PACK], BF16, name="h_bf", align_bytes=64)
-        h_codes = [keep.tile([P, P], U32, name="h_codes%d" % t, align_bytes=64) for t in range(PACK)]
-        h_sc = [keep.tile([P, P], U8, name="h_sc%d" % t, align_bytes=64) for t in range(PACK)]
+        h_codes = keep.tile([P, H], U32, name="h_codes", align_bytes=64)
+        h_sc = keep.tile([P, H], U8, name="h_sc", align_bytes=64)
         picked_words = [keep.tile([P, P * D], U32, name="picked_words%d" % b) for b in range(VB)]
         x_codes = [keep.tile([P, D, P], U32, name="x_codes%d" % b, align_bytes=64) for b in range(VB)]
 
@@ -79,27 +78,33 @@ def tile_picked_ycavqe_conc_p_kernel(tc, x_words, x_scales, hT, unit, w1, offs, 
         def deal(b):
             nc.vector.tensor_copy(x_codes[b][:], picked_words[b][:].rearrange("p (v d) -> p d v", d=D))
 
-        def cast_views(a):
-            m = slice(a * (P // 2), (a + 1) * (P // 2))
+        def cast_views(a, lo, hi):
+            first = a * (P // 2)
             return (
-                h_bf[:, :, m, :].rearrange("p t m j -> p m t j"),
-                h_raw[a][:].rearrange("p j (m t) -> p m t j", t=PACK),
+                h_bf[:, :, first + lo : first + hi, :].rearrange("p t m j -> p m t j"),
+                h_raw[a][:, :, PACK * lo : PACK * hi].rearrange("p j (m t) -> p m t j", t=PACK),
             )
 
-        def quant_h(t):
-            nc.vector.quantize_mx(h_codes[t][:].bitcast(FP8X4), h_sc[t][:], h_bf[:, t].rearrange("p m j -> p (m j)"))
+        def quant_h(lo, hi):
+            nc.vector.quantize_mx(
+                h_codes[:, lo * P : hi * P].bitcast(FP8X4),
+                h_sc[:, lo * P : hi * P],
+                h_bf[:, lo:hi].rearrange("p t m j -> p (t m j)"),
+            )
 
         pick(0)
-        nc.scalar.copy(*cast_views(0))
+        nc.scalar.copy(*cast_views(0, 0, P // 2))
+        nc.scalar.copy(*cast_views(1, 0, P // 2))
         deal(0)
         pick(1)
-        nc.vector.tensor_copy(*cast_views(1))
-        quant_h(0)
         deal(1)
-        for t in range(1, PACK):
-            quant_h(t)
+        quant_h(0, 1)
+        quant_h(1, PACK)
 
-        w_bf = keep.tile([P, N, PACK], BF16, name="w_bf", align_bytes=64)
+        w_bf = h_bf[:, 2:].rearrange("p t m j -> p (t m j)")
+        nc.gpsimd.tensor_scalar(
+            w_bf.rearrange("p (n j) -> p n j", j=PACK), w_raw[:].rearrange("p j n -> p n j"), 1.0, 0.0, ALU.mult, ALU.add
+        )
         w_codes = keep.tile([P, N], U32, name="w_codes", align_bytes=64)
         w_sc = keep.tile([P, N], U8, name="w_sc", align_bytes=64)
 
@@ -122,25 +127,33 @@ def tile_picked_ycavqe_conc_p_kernel(tc, x_words, x_scales, hT, unit, w1, offs, 
                     y[:, d, :],
                     lhsT=x_codes[b][:, d, :].bitcast(FP8X4),
                     lhsT_scale=x_sc[:, b, d, :],
-                    rhs=h_codes[t][:].bitcast(FP8X4),
-                    rhs_scale=h_sc[t][:],
+                    rhs=h_codes[:, t * P : (t + 1) * P].bitcast(FP8X4),
+                    rhs_scale=h_sc[:, t * P : (t + 1) * P],
                     start=True,
                     stop=True,
                 )
             y_src[n] = y
 
+        tops = {}
+
+        def largest(n):
+            if n == last:
+                tops[n] = ey_all[HELD_FROM][:, 0, :]
+            else:
+                top_tile = work.tile([P, P], F32, name="top_tile")
+                tops[n] = top_tile[:]
+            nc.vector.tensor_reduce(tops[n], y_src[n][:].rearrange("p d i -> p i d"), AX.X, ALU.max)
+
         def softmax_terms(n):
             y = y_src[n]
-            top = work.tile([P, P], F32, name="top")
             if n >= last - 1:
                 z = log_sum[:, last - n, :].rearrange("p (d i) -> p d i", d=D)
             else:
                 z_tile = work.tile([P, D, P], F32, name="z_tile")
                 z = z_tile[:]
-            nc.vector.tensor_reduce(top[:], y[:].rearrange("p d i -> p i d"), AX.X, ALU.max)
-            nc.vector.tensor_tensor(z, y[:], top[:].unsqueeze(1).to_broadcast([P, D, P]), ALU.subtract)
+            nc.vector.tensor_tensor(z, y[:], tops[n].unsqueeze(1).to_broadcast([P, D, P]), ALU.subtract)
             nc.scalar.activation(e_all[n][:], z, ACT.Exp)
-            if EARLY <= n < HELD_FROM:
+            if n < HELD_FROM:
                 y_sb = keep.tile([P, D, P], F32, name="y_sb%d" % n)
                 nc.scalar.copy(y_sb[:], y[:])
                 y_src[n] = y_sb
@@ -149,73 +162,76 @@ def tile_picked_ycavqe_conc_p_kernel(tc, x_words, x_scales, hT, unit, w1, offs, 
             for d in range(D):
                 nc.tensor.matmul(dst, lhsT=src[:, d, :], rhs=ident[:], start=d == 0, stop=d == D - 1, is_transpose=True)
 
-        def weigh(n):
-            nc.vector.tensor_tensor(ey_all[n][:], y_src[n][:], e_all[n][:], ALU.mult)
-
-        def sums(n):
-            t, b = order[n]
-            if n < EARLY:
-                weigh(n)
-            ee = work.tile([P, D, P], F32, name="ee")
-            nc.scalar.activation(ee[:], e_all[n][:], ACT.Square)
-            add_up(sum_e[b][:, t, :], e_all[n])
-            add_up(sum_ee[t // 2][:, t % 2, b * P : (b + 1) * P], ee)
-
         for n in range(HELD_FROM):
             scores(n)
-        softmax_terms(0)
+        largest(0)
         for n in range(len(order)):
+            t, b = order[n]
             if n + 1 < len(order):
-                softmax_terms(n + 1)
-            sums(n)
+                largest(n + 1)
+            softmax_terms(n)
             if n + HELD_FROM < len(order):
                 scores(n + HELD_FROM)
+            add_up(sum_e[b][:, t, :], e_all[n])
 
         for b in range(VB):
             nc.scalar.activation(log_sum[:, b, :], sum_e[b][:].rearrange("p t v -> p (t v)"), ACT.Ln)
-
-        for n in (4, 5, 2, 3, 6, 7):
-            weigh(n)
-        sum_ey = [py.tile([P, D, P], F32, name="y") for g in range(2)]
-        for n in (0, 1, 4, 5, 2, 3, 6, 7):
-            t, b = order[n]
-            add_up(sum_ey[t // 2][:, 2 * (t % 2) + b, :], ey_all[n])
-        nc.vector.tensor_copy(
-            w_bf[:].rearrange("p (c i) j -> p c j i", i=4), w_raw[:].rearrange("p j (c i) -> p c j i", i=4)
-        )
-        nc.vector.quantize_mx(w_codes[:].bitcast(FP8X4), w_sc[:], w_bf[:].rearrange("p n j -> p (n j)"))
-
-        windows = [keep.tile([P, 2 * V], F32, name="window%d" % t) for t in range(PACK)]
         inv3 = [keep.tile([P, VB, P], F32, name="inv3_%d" % t) for t in range(PACK)]
         for t in range(PACK):
             nc.scalar.activation(inv3[t][:], log_sum[:, :, t * P : (t + 1) * P], ACT.Exp, scale=-3.0)
 
-        def scaled(t):
-            nc.vector.scalar_tensor_tensor(
-                windows[t][:, V:],
-                sum_ey[t // 2][:, 2 * (t % 2) : 2 * (t % 2) + 2, :].rearrange("p b v -> p (b v)"),
-                unit_sb[:, t : t + 1],
-                inv3[t][:].rearrange("p b v -> p (b v)"),
-                ALU.mult,
-                ALU.mult,
-            )
+        ee_all = [keep.tile([P, D, P], F32, name="ee%d" % n) for n in range(len(order))]
+        for n in range(len(order)):
+            if n < HELD_FROM:
+                nc.gpsimd.tensor_tensor(ey_all[n][:], y_src[n][:], e_all[n][:], ALU.mult)
+                nc.scalar.activation(ee_all[n][:], e_all[n][:], ACT.Square)
+            else:
+                nc.vector.tensor_tensor(ey_all[n][:], y_src[n][:], e_all[n][:], ALU.mult)
+                nc.gpsimd.tensor_tensor(ee_all[n][:], e_all[n][:], e_all[n][:], ALU.mult)
+        sum_ey = [py.tile([P, D, P], F32, name="y") for g in range(2)]
 
-        def finish(t):
-            nc.vector.tensor_tensor(windows[t][:, :V], sum_ee[t // 2][:, t % 2, :], windows[t][:, V:], ALU.mult)
+        def add_ee(n):
+            t, b = order[n]
+            add_up(sum_ee[t // 2][:, t % 2, b * P : (b + 1) * P], ee_all[n])
+
+        def add_ey(n):
+            t, b = order[n]
+            add_up(sum_ey[t // 2][:, 2 * (t % 2) + b, :], ey_all[n])
+
+        for n in range(last):
+            add_ee(n)
+        for n in range(last):
+            add_ey(n)
+        add_ee(last)
+        add_ey(last)
+
+        windows = [keep.tile([P, 2 * V], F32, name="window%d" % t) for t in range(PACK)]
+        scaled = [keep.tile([P, V], F32, name="scaled%d" % t) for t in range(PACK)]
+        for g in range(2):
+            for t in (2 * g, 2 * g + 1):
+                nc.vector.tensor_scalar(scaled[t][:], sum_ee[g][:, t % 2, :], unit_sb[:, t : t + 1], None, ALU.mult)
+            for t in (2 * g, 2 * g + 1):
+                nc.vector.tensor_tensor(
+                    windows[t][:, V:],
+                    sum_ey[g][:, 2 * (t % 2) : 2 * (t % 2) + 2, :].rearrange("p b v -> p (b v)"),
+                    scaled[t][:],
+                    ALU.mult,
+                )
+            if g == 0:
+                nc.vector.quantize_mx(w_codes[:].bitcast(FP8X4), w_sc[:], w_bf)
+        for t in range(PACK):
+            nc.vector.tensor_tensor(
+                windows[t][:, :V], windows[t][:, V:], inv3[t][:].rearrange("p b v -> p (b v)"), ALU.mult
+            )
 
         def fetch(t, r):
             cols = HALF // 16
             src = windows[t][:].indirect(use_sb[:, r * cols : (r + 1) * cols])
-            if r == 0 and t >= 2:
+            if t >= 2 + r:
                 nc.vector.tensor_copy(hid_planes[r][:, t, :], src)
             else:
                 nc.scalar.activation(hid_planes[r][:, t, :], src, ACT.Copy)
 
-        scaled(0)
-        for t in range(PACK):
-            if t + 1 < PACK:
-                scaled(t + 1)
-            finish(t)
         for r in range(2):
             for t in range(PACK):
                 fetch(t, r)
@@ -241,5 +257,9 @@ def tile_picked_ycavqe_conc_p_kernel(tc, x_words, x_scales, hT, unit, w1, offs, 
                     stop=True,
                 )
                 res = keep.tile([P, HALF], F32, name="res%d_%d" % (r, mt))
-                nc.scalar.copy(res[:], acc_cols)
-                nc.sync.dma_start(out[mt * P : (mt + 1) * P, r * HALF : (r + 1) * HALF], res[:])
+                if r == 1 and mt == 1:
+                    nc.vector.tensor_copy(res[:], acc_cols)
+                else:
+                    nc.scalar.copy(res[:], acc_cols)
+                queue = nc.scalar if r == 1 and mt == 0 else nc.sync
+                queue.dma_start(out[mt * P : (mt + 1) * P, r * HALF : (r + 1) * HALF], res[:])

@@ -21,7 +21,11 @@ P = 128
 PACK = 4
 VB = V // P
 HALF = U // 2
-HELD_FROM = 4
+Y_BANKS = 4
+PAIRED_SUMS = 5
+SCALAR_SQUARES = 5
+EARLY_PLANES = 2
+E, EE, EY = 0, 1, 2
 
 
 def tile_picked_ycavqe_conc_p_kernel(tc, x_words, x_scales, hT, unit, w1, offs, use, out):
@@ -29,8 +33,8 @@ def tile_picked_ycavqe_conc_p_kernel(tc, x_words, x_scales, hT, unit, w1, offs, 
     with ExitStack() as ctx:
         keep = ctx.enter_context(tc.tile_pool(name="keep", bufs=1))
         work = ctx.enter_context(tc.tile_pool(name="work", bufs=3))
-        py = ctx.enter_context(tc.psum_pool(name="py", bufs=4))
-        ps = ctx.enter_context(tc.psum_pool(name="ps", bufs=1))
+        py = ctx.enter_context(tc.psum_pool(name="py", bufs=Y_BANKS))
+        ps = ctx.enter_context(tc.psum_pool(name="ps", bufs=2))
 
         offs_sb = keep.tile([P, S // 16], U16, name="offs_sb")
         use_sb = keep.tile([P, U // 16], U16, name="use_sb")
@@ -63,11 +67,13 @@ def tile_picked_ycavqe_conc_p_kernel(tc, x_words, x_scales, hT, unit, w1, offs, 
         nc.vector.tensor_copy(picked_scales[:], table_scales[:].indirect(offs_sb[:]))
         nc.vector.tensor_copy(x_sc[:], picked_scales[:].rearrange("p (b v d) -> p b d v", b=VB, d=D))
 
-        h_bf = keep.tile([P, PACK, P, PACK], BF16, name="h_bf", align_bytes=64)
+        h_bf = [
+            keep.tile([P, 2, P, PACK], BF16, name="h_bf%d" % g, tag="stage%d" % g, align_bytes=64) for g in range(2)
+        ]
         h_codes = keep.tile([P, H], U32, name="h_codes", align_bytes=64)
         h_sc = keep.tile([P, H], U8, name="h_sc", align_bytes=64)
         picked_words = [keep.tile([P, P * D], U32, name="picked_words%d" % b) for b in range(VB)]
-        x_codes = [keep.tile([P, D, P], U32, name="x_codes%d" % b, align_bytes=64) for b in range(VB)]
+        x_codes = {}
 
         def pick(b):
             cols = P * D // 16
@@ -75,49 +81,47 @@ def tile_picked_ycavqe_conc_p_kernel(tc, x_words, x_scales, hT, unit, w1, offs, 
                 picked_words[b][:], table_words[:].bitcast(U32).indirect(offs_sb[:, b * cols : (b + 1) * cols])
             )
 
-        def deal(b):
+        def deal(b, tag):
+            x_codes[b] = keep.tile([P, D, P], U32, name="x_codes%d" % b, tag=tag, align_bytes=64)
             nc.vector.tensor_copy(x_codes[b][:], picked_words[b][:].rearrange("p (v d) -> p d v", d=D))
 
-        def cast_views(a, lo, hi):
-            first = a * (P // 2)
-            return (
-                h_bf[:, :, first + lo : first + hi, :].rearrange("p t m j -> p m t j"),
-                h_raw[a][:, :, PACK * lo : PACK * hi].rearrange("p j (m t) -> p m t j", t=PACK),
+        def cast_h(a, g):
+            frames = slice(a * (P // 2), (a + 1) * (P // 2))
+            nc.scalar.copy(
+                h_bf[g][:, :, frames, :].rearrange("p t m j -> p m t j"),
+                h_raw[a][:].rearrange("p j (m t) -> p m t j", t=PACK)[:, :, 2 * g : 2 * g + 2, :],
             )
 
         def quant_h(lo, hi):
             nc.vector.quantize_mx(
                 h_codes[:, lo * P : hi * P].bitcast(FP8X4),
                 h_sc[:, lo * P : hi * P],
-                h_bf[:, lo:hi].rearrange("p t m j -> p (t m j)"),
+                h_bf[lo // 2][:, lo % 2 : lo % 2 + hi - lo].rearrange("p t m j -> p (t m j)"),
             )
 
         pick(0)
-        nc.scalar.copy(*cast_views(0, 0, P // 2))
-        nc.scalar.copy(*cast_views(1, 0, P // 2))
-        deal(0)
+        for a in range(2):
+            for g in range(2):
+                cast_h(a, g)
+        deal(0, "x_codes0")
         pick(1)
-        deal(1)
         quant_h(0, 1)
-        quant_h(1, PACK)
+        quant_h(1, 2)
+        deal(1, "stage0")
+        quant_h(2, PACK)
 
-        w_bf = h_bf[:, 2:].rearrange("p t m j -> p (t m j)")
-        nc.gpsimd.tensor_scalar(
-            w_bf.rearrange("p (n j) -> p n j", j=PACK), w_raw[:].rearrange("p j n -> p n j"), 1.0, 0.0, ALU.mult, ALU.add
-        )
+        w_bf = keep.tile([P, N, PACK], BF16, name="w_bf", align_bytes=64)
         w_codes = keep.tile([P, N], U32, name="w_codes", align_bytes=64)
         w_sc = keep.tile([P, N], U8, name="w_sc", align_bytes=64)
-
-        hid_planes = [keep.tile([P, PACK, HALF], BF16, name="hid_planes%d" % r) for r in range(2)]
+        nc.scalar.copy(w_bf[:].rearrange("p (c i) j -> p c j i", i=4), w_raw[:].rearrange("p j (c i) -> p c j i", i=4))
 
         order = [(t, b) for t in range(PACK) for b in range(VB)]
         last = len(order) - 1
-        sum_e = [ps.tile([P, PACK, P], F32, name="sum_e%d" % b) for b in range(VB)]
-        sum_ee = [ps.tile([P, 2, V], F32, name="sum_ee%d" % g) for g in range(2)]
-        log_sum = keep.tile([P, VB, D * P], F32, name="log_sum")
-        y_src = {}
-        e_all = [keep.tile([P, D, P], F32, name="e%d" % n) for n in range(len(order))]
-        ey_all = [keep.tile([P, D, P], F32, name="ey%d" % n) for n in range(len(order))]
+        terms = [keep.tile([P, 3, D, P], F32, name="terms%d" % n) for n in range(len(order))]
+        inv3 = keep.tile([P, PACK, V], F32, name="inv3")
+        sixth = [keep.tile([P, V], F32, name="sixth%d" % t) for t in range(PACK)]
+        windows = [keep.tile([P, 2 * V], F32, name="window%d" % t) for t in range(PACK)]
+        y_banks, tops, sum_e, sum_rest = {}, {}, {}, {}
 
         def scores(n):
             t, b = order[n]
@@ -132,102 +136,108 @@ def tile_picked_ycavqe_conc_p_kernel(tc, x_words, x_scales, hT, unit, w1, offs, 
                     start=True,
                     stop=True,
                 )
-            y_src[n] = y
-
-        tops = {}
+            y_banks[n] = y
 
         def largest(n):
-            if n == last:
-                tops[n] = ey_all[HELD_FROM][:, 0, :]
-            else:
-                top_tile = work.tile([P, P], F32, name="top_tile")
-                tops[n] = top_tile[:]
-            nc.vector.tensor_reduce(tops[n], y_src[n][:].rearrange("p d i -> p i d"), AX.X, ALU.max)
+            top = work.tile([P, P], F32, name="top")
+            nc.vector.tensor_reduce(top[:], y_banks[n][:].rearrange("p d i -> p i d"), AX.X, ALU.max)
+            tops[n] = top
 
-        def softmax_terms(n):
-            y = y_src[n]
-            if n >= last - 1:
-                z = log_sum[:, last - n, :].rearrange("p (d i) -> p d i", d=D)
+        def exponentials(n):
+            if n == last:
+                z = inv3[:, :, :P]
             else:
                 z_tile = work.tile([P, D, P], F32, name="z_tile")
                 z = z_tile[:]
-            nc.vector.tensor_tensor(z, y[:], tops[n].unsqueeze(1).to_broadcast([P, D, P]), ALU.subtract)
-            nc.scalar.activation(e_all[n][:], z, ACT.Exp)
-            if n < HELD_FROM:
-                y_sb = keep.tile([P, D, P], F32, name="y_sb%d" % n)
-                nc.scalar.copy(y_sb[:], y[:])
-                y_src[n] = y_sb
+            nc.vector.tensor_tensor(z, y_banks[n][:], tops[n][:].unsqueeze(1).to_broadcast([P, D, P]), ALU.subtract)
+            nc.scalar.activation(terms[n][:, E], z, ACT.Exp)
 
         def add_up(dst, src):
-            for d in range(D):
-                nc.tensor.matmul(dst, lhsT=src[:, d, :], rhs=ident[:], start=d == 0, stop=d == D - 1, is_transpose=True)
+            count = src.shape[1]
+            for d in range(count):
+                nc.tensor.matmul(
+                    dst, lhsT=src[:, d, :], rhs=ident[:], start=d == 0, stop=d == count - 1, is_transpose=True
+                )
 
-        for n in range(HELD_FROM):
+        def add_pairs(src):
+            pairs = work.tile([P, D // 2, P], F32, name="pairs", bufs=4)
+            nc.gpsimd.tensor_tensor(pairs[:], src[:, : D // 2, :], src[:, D // 2 :, :], ALU.add)
+            return pairs[:]
+
+        def sum_shares(n):
+            t, b = order[n]
+            if b == 0:
+                sum_e[t] = ps.tile([P, V], F32, name="sum_e")
+                sum_rest[t] = ps.tile([P, 2, V], F32, name="sum_rest")
+            cols = slice(b * P, (b + 1) * P)
+            e, ee = terms[n][:, E], terms[n][:, EE]
+            add_up(sum_e[t][:, cols], add_pairs(e) if n < PAIRED_SUMS else e)
+            if n < SCALAR_SQUARES:
+                nc.scalar.activation(ee, e, ACT.Square)
+                add_up(sum_rest[t][:, 0, cols], add_pairs(ee))
+            else:
+                nc.gpsimd.tensor_tensor(ee, e, e, ALU.mult)
+
+        def sum_weighted(n):
+            t, b = order[n]
+            nc.vector.tensor_tensor(terms[n][:, EY], y_banks[n][:], terms[n][:, E], ALU.mult)
+            if n + Y_BANKS <= last:
+                scores(n + Y_BANKS)
+            add_up(sum_rest[t][:, 1, b * P : (b + 1) * P], terms[n][:, EY])
+
+        def sixth_power(t):
+            second = work.tile([P, V], F32, name="second")
+            fourth = work.tile([P, V], F32, name="fourth")
+            nc.scalar.activation(second[:], sum_e[t][:], ACT.Square)
+            nc.scalar.activation(fourth[:], second[:], ACT.Square)
+            engine = nc.gpsimd if t < EARLY_PLANES else nc.vector
+            engine.tensor_tensor(sixth[t][:], second[:], fourth[:], ALU.mult)
+
+        def numerator(t):
+            scaled = work.tile([P, V], F32, name="scaled")
+            nc.scalar.activation(scaled[:], sum_rest[t][:, 0, :], ACT.Copy, scale=unit_sb[:, t : t + 1])
+            nc.vector.tensor_tensor(windows[t][:, V:], sum_rest[t][:, 1, :], scaled[:], ALU.mult)
+
+        def finish(t):
+            nc.scalar.activation(inv3[:, t, :], sixth[t][:], ACT.Abs_reciprocal_sqrt)
+            if t < EARLY_PLANES:
+                nc.vector.tensor_tensor(windows[t][:, :V], windows[t][:, V:], inv3[:, t, :], ALU.mult)
+            else:
+                nc.vector.tensor_tensor(windows[t][:, V:], sum_rest[t][:, 0, :], inv3[:, t, :], ALU.mult)
+                nc.vector.scalar_tensor_tensor(
+                    windows[t][:, :V], sum_rest[t][:, 1, :], unit_sb[:, t : t + 1], windows[t][:, V:], ALU.mult, ALU.mult
+                )
+
+        for n in range(Y_BANKS):
             scores(n)
         largest(0)
         for n in range(len(order)):
             t, b = order[n]
-            if n + 1 < len(order):
+            if n < last:
                 largest(n + 1)
-            softmax_terms(n)
-            if n + HELD_FROM < len(order):
-                scores(n + HELD_FROM)
-            add_up(sum_e[b][:, t, :], e_all[n])
-
-        for b in range(VB):
-            nc.scalar.activation(log_sum[:, b, :], sum_e[b][:].rearrange("p t v -> p (t v)"), ACT.Ln)
-        inv3 = [keep.tile([P, VB, P], F32, name="inv3_%d" % t) for t in range(PACK)]
-        for t in range(PACK):
-            nc.scalar.activation(inv3[t][:], log_sum[:, :, t * P : (t + 1) * P], ACT.Exp, scale=-3.0)
-
-        ee_all = [keep.tile([P, D, P], F32, name="ee%d" % n) for n in range(len(order))]
-        for n in range(len(order)):
-            if n < HELD_FROM:
-                nc.gpsimd.tensor_tensor(ey_all[n][:], y_src[n][:], e_all[n][:], ALU.mult)
-                nc.scalar.activation(ee_all[n][:], e_all[n][:], ACT.Square)
-            else:
-                nc.vector.tensor_tensor(ey_all[n][:], y_src[n][:], e_all[n][:], ALU.mult)
-                nc.gpsimd.tensor_tensor(ee_all[n][:], e_all[n][:], e_all[n][:], ALU.mult)
-        sum_ey = [py.tile([P, D, P], F32, name="y") for g in range(2)]
-
-        def add_ee(n):
+            exponentials(n)
+            if 0 < n <= Y_BANKS:
+                sum_weighted(n - 1)
+            sum_shares(n)
+            if b == VB - 1:
+                sixth_power(t)
+            elif 0 < t <= EARLY_PLANES:
+                numerator(t - 1)
+        for n in range(Y_BANKS, len(order)):
+            sum_weighted(n)
+        for n in range(SCALAR_SQUARES, len(order)):
             t, b = order[n]
-            add_up(sum_ee[t // 2][:, t % 2, b * P : (b + 1) * P], ee_all[n])
-
-        def add_ey(n):
-            t, b = order[n]
-            add_up(sum_ey[t // 2][:, 2 * (t % 2) + b, :], ey_all[n])
-
-        for n in range(last):
-            add_ee(n)
-        for n in range(last):
-            add_ey(n)
-        add_ee(last)
-        add_ey(last)
-
-        windows = [keep.tile([P, 2 * V], F32, name="window%d" % t) for t in range(PACK)]
-        scaled = [keep.tile([P, V], F32, name="scaled%d" % t) for t in range(PACK)]
-        for g in range(2):
-            for t in (2 * g, 2 * g + 1):
-                nc.vector.tensor_scalar(scaled[t][:], sum_ee[g][:, t % 2, :], unit_sb[:, t : t + 1], None, ALU.mult)
-            for t in (2 * g, 2 * g + 1):
-                nc.vector.tensor_tensor(
-                    windows[t][:, V:],
-                    sum_ey[g][:, 2 * (t % 2) : 2 * (t % 2) + 2, :].rearrange("p b v -> p (b v)"),
-                    scaled[t][:],
-                    ALU.mult,
-                )
-            if g == 0:
-                nc.vector.quantize_mx(w_codes[:].bitcast(FP8X4), w_sc[:], w_bf)
+            add_up(sum_rest[t][:, 0, b * P : (b + 1) * P], terms[n][:, EE])
+        nc.vector.quantize_mx(w_codes[:].bitcast(FP8X4), w_sc[:], w_bf[:].rearrange("p n j -> p (n j)"))
         for t in range(PACK):
-            nc.vector.tensor_tensor(
-                windows[t][:, :V], windows[t][:, V:], inv3[t][:].rearrange("p b v -> p (b v)"), ALU.mult
-            )
+            finish(t)
+
+        hid_planes = [keep.tile([P, PACK, HALF], BF16, name="hid_planes%d" % r) for r in range(2)]
 
         def fetch(t, r):
             cols = HALF // 16
             src = windows[t][:].indirect(use_sb[:, r * cols : (r + 1) * cols])
-            if t >= 2 + r:
+            if t == PACK - 1:
                 nc.vector.tensor_copy(hid_planes[r][:, t, :], src)
             else:
                 nc.scalar.activation(hid_planes[r][:, t, :], src, ACT.Copy)

@@ -22,8 +22,7 @@ PACK = 4
 VB = V // P
 HALF = U // 2
 Y_BANKS = 4
-PAIRED_SUMS = 5
-SCALAR_SQUARES = 5
+SCALAR_SQUARES = 6
 EARLY_PLANES = 2
 E, EE, EY = 0, 1, 2
 
@@ -159,11 +158,6 @@ def tile_picked_ycavqe_conc_p_kernel(tc, x_words, x_scales, hT, unit, w1, offs, 
                     dst, lhsT=src[:, d, :], rhs=ident[:], start=d == 0, stop=d == count - 1, is_transpose=True
                 )
 
-        def add_pairs(src):
-            pairs = work.tile([P, D // 2, P], F32, name="pairs", bufs=4)
-            nc.gpsimd.tensor_tensor(pairs[:], src[:, : D // 2, :], src[:, D // 2 :, :], ALU.add)
-            return pairs[:]
-
         def sum_shares(n):
             t, b = order[n]
             if b == 0:
@@ -171,12 +165,10 @@ def tile_picked_ycavqe_conc_p_kernel(tc, x_words, x_scales, hT, unit, w1, offs, 
                 sum_rest[t] = ps.tile([P, 2, V], F32, name="sum_rest")
             cols = slice(b * P, (b + 1) * P)
             e, ee = terms[n][:, E], terms[n][:, EE]
-            add_up(sum_e[t][:, cols], add_pairs(e) if n < PAIRED_SUMS else e)
+            add_up(sum_e[t][:, cols], e)
             if n < SCALAR_SQUARES:
                 nc.scalar.activation(ee, e, ACT.Square)
-                add_up(sum_rest[t][:, 0, cols], add_pairs(ee))
-            else:
-                nc.gpsimd.tensor_tensor(ee, e, e, ALU.mult)
+                add_up(sum_rest[t][:, 0, cols], ee)
 
         def sum_weighted(n):
             t, b = order[n]
@@ -187,11 +179,10 @@ def tile_picked_ycavqe_conc_p_kernel(tc, x_words, x_scales, hT, unit, w1, offs, 
 
         def sixth_power(t):
             second = work.tile([P, V], F32, name="second")
-            fourth = work.tile([P, V], F32, name="fourth")
+            third = work.tile([P, V], F32, name="third")
             nc.scalar.activation(second[:], sum_e[t][:], ACT.Square)
-            nc.scalar.activation(fourth[:], second[:], ACT.Square)
-            engine = nc.gpsimd if t < EARLY_PLANES else nc.vector
-            engine.tensor_tensor(sixth[t][:], second[:], fourth[:], ALU.mult)
+            nc.vector.tensor_tensor(third[:], sum_e[t][:], second[:], ALU.mult)
+            nc.scalar.activation(sixth[t][:], third[:], ACT.Square)
 
         def numerator(t):
             scaled = work.tile([P, V], F32, name="scaled")
@@ -225,6 +216,8 @@ def tile_picked_ycavqe_conc_p_kernel(tc, x_words, x_scales, hT, unit, w1, offs, 
                 numerator(t - 1)
         for n in range(Y_BANKS, len(order)):
             sum_weighted(n)
+            if n >= SCALAR_SQUARES:
+                nc.vector.tensor_tensor(terms[n][:, EE], terms[n][:, E], terms[n][:, E], ALU.mult)
         for n in range(SCALAR_SQUARES, len(order)):
             t, b = order[n]
             add_up(sum_rest[t][:, 0, b * P : (b + 1) * P], terms[n][:, EE])
@@ -237,7 +230,7 @@ def tile_picked_ycavqe_conc_p_kernel(tc, x_words, x_scales, hT, unit, w1, offs, 
         def fetch(t, r):
             cols = HALF // 16
             src = windows[t][:].indirect(use_sb[:, r * cols : (r + 1) * cols])
-            if t == PACK - 1:
+            if t == 0:
                 nc.vector.tensor_copy(hid_planes[r][:, t, :], src)
             else:
                 nc.scalar.activation(hid_planes[r][:, t, :], src, ACT.Copy)

from contextlib import ExitStack

import concourse.mybir as mybir
from concourse.masks import make_identity

K, T, S, D, N, H, V, U = 512, 4096, 1024, 4, 256, 512, 256, 512
FLOPS = 2 * K * H * S + 2 * H * N * U

F32 = mybir.dt.float32
BF16 = mybir.dt.bfloat16
I32 = mybir.dt.int32
U32 = mybir.dt.uint32
U16 = mybir.dt.uint16
U8 = mybir.dt.uint8
FP8X4 = mybir.dt.float8_e4m3fn_x4
ALU = mybir.AluOpType
ACT = mybir.ActivationFunctionType
AX = mybir.AxisListType

P = 128
PACK = 4
VB = V // P
HALF = U // 2
Y_BANKS = 4
SCALAR_SQUARES = 6
EARLY_PLANES = 2
E, EE, EY = 0, 1, 2


def tile_picked_ycavqe_conc_p_kernel(tc, x_words, x_scales, hT, unit, w1, offs, use, out):
    nc = tc.nc
    with ExitStack() as ctx:
        keep = ctx.enter_context(tc.tile_pool(name="keep", bufs=1))
        work = ctx.enter_context(tc.tile_pool(name="work", bufs=3))
        py = ctx.enter_context(tc.psum_pool(name="py", bufs=Y_BANKS))
        ps = ctx.enter_context(tc.psum_pool(name="ps", bufs=2))

        offs_sb = keep.tile([P, S // 16], U16, name="offs_sb")
        use_sb = keep.tile([P, U // 16], U16, name="use_sb")
        table_words = keep.tile([P, T], I32, name="table_words")
        table_scales = keep.tile([P, T], U8, name="table_scales")
        h_raw = [keep.tile([P, PACK, H // 2], F32, name="h_raw%d" % a) for a in range(2)]
        w_raw = keep.tile([P, PACK, N], F32, name="w_raw")
        unit_sb = keep.tile([P, PACK], F32, name="unit_sb")
        ident = keep.tile([P, P], F32, name="ident")

        nc.vector.memset(table_scales[:].bitcast(I32), 0)
        nc.sync.dma_start(offs_sb[:], offs)
        words_view = x_words[0].rearrange("p n t -> p (n t)").bitcast(I32)
        nc.sync.dma_start(table_words[:, : T // 4], words_view[:, : T // 4])
        for q in range(4):
            nc.sync.dma_start(
                table_scales[32 * q : 32 * q + 4, :].bitcast(I32), x_scales[0, 4 * q : 4 * q + 4, :].bitcast(I32)
            )
        nc.sync.dma_start(table_words[:, T // 4 :], words_view[:, T // 4 :])
        h_view = hT.rearrange("(p j) c -> p j c", j=PACK)
        for a in range(2):
            nc.sync.dma_start(h_raw[a][:], h_view[:, :, a * (H // 2) : (a + 1) * (H // 2)])
        nc.sync.dma_start(w_raw[:], w1.rearrange("(p j) n -> p j n", j=PACK))
        nc.sync.dma_start(use_sb[:], use)
        nc.sync.dma_start(unit_sb[:], unit.rearrange("(p t) o -> p (t o)", t=PACK))
        make_identity(nc, ident[:])

        picked_scales = keep.tile([P, S], U8, name="picked_scales")
        x_sc = keep.tile([P, VB, D, P], U8, name="x_sc", align_bytes=64)
        nc.vector.tensor_copy(picked_scales[:], table_scales[:].indirect(offs_sb[:]))
        nc.vector.tensor_copy(x_sc[:], picked_scales[:].rearrange("p (b v d) -> p b d v", b=VB, d=D))

        h_bf = [
            keep.tile([P, 2, P, PACK], BF16, name="h_bf%d" % g, tag="stage%d" % g, align_bytes=64) for g in range(2)
        ]
        h_codes = keep.tile([P, H], U32, name="h_codes", align_bytes=64)
        h_sc = keep.tile([P, H], U8, name="h_sc", align_bytes=64)
        picked_words = [keep.tile([P, P * D], U32, name="picked_words%d" % b) for b in range(VB)]
        x_codes = {}

        def pick(b):
            cols = P * D // 16
            nc.vector.tensor_copy(
                picked_words[b][:], table_words[:].bitcast(U32).indirect(offs_sb[:, b * cols : (b + 1) * cols])
            )

        def deal(b, tag):
            x_codes[b] = keep.tile([P, D, P], U32, name="x_codes%d" % b, tag=tag, align_bytes=64)
            nc.vector.tensor_copy(x_codes[b][:], picked_words[b][:].rearrange("p (v d) -> p d v", d=D))

        def cast_h(a, g):
            frames = slice(a * (P // 2), (a + 1) * (P // 2))
            nc.scalar.copy(
                h_bf[g][:, :, frames, :].rearrange("p t m j -> p m t j"),
                h_raw[a][:].rearrange("p j (m t) -> p m t j", t=PACK)[:, :, 2 * g : 2 * g + 2, :],
            )

        def quant_h(lo, hi):
            nc.vector.quantize_mx(
                h_codes[:, lo * P : hi * P].bitcast(FP8X4),
                h_sc[:, lo * P : hi * P],
                h_bf[lo // 2][:, lo % 2 : lo % 2 + hi - lo].rearrange("p t m j -> p (t m j)"),
            )

        pick(0)
        for a in range(2):
            for g in range(2):
                cast_h(a, g)
        deal(0, "x_codes0")
        pick(1)
        quant_h(0, 1)
        quant_h(1, 2)
        deal(1, "stage0")
        quant_h(2, PACK)

        w_bf = keep.tile([P, N, PACK], BF16, name="w_bf", align_bytes=64)
        w_codes = keep.tile([P, N], U32, name="w_codes", align_bytes=64)
        w_sc = keep.tile([P, N], U8, name="w_sc", align_bytes=64)
        nc.scalar.copy(w_bf[:].rearrange("p (c i) j -> p c j i", i=4), w_raw[:].rearrange("p j (c i) -> p c j i", i=4))

        order = [(t, b) for t in range(PACK) for b in range(VB)]
        last = len(order) - 1
        terms = [keep.tile([P, 3, D, P], F32, name="terms%d" % n) for n in range(len(order))]
        inv3 = keep.tile([P, PACK, V], F32, name="inv3")
        sixth = [keep.tile([P, V], F32, name="sixth%d" % t) for t in range(PACK)]
        windows = [keep.tile([P, 2 * V], F32, name="window%d" % t) for t in range(PACK)]
        y_banks, tops, sum_e, sum_rest = {}, {}, {}, {}

        def scores(n):
            t, b = order[n]
            y = py.tile([P, D, P], F32, name="y")
            for d in range(D):
                nc.tensor.matmul_mx(
                    y[:, d, :],
                    lhsT=x_codes[b][:, d, :].bitcast(FP8X4),
                    lhsT_scale=x_sc[:, b, d, :],
                    rhs=h_codes[:, t * P : (t + 1) * P].bitcast(FP8X4),
                    rhs_scale=h_sc[:, t * P : (t + 1) * P],
                    start=True,
                    stop=True,
                )
            y_banks[n] = y

        def largest(n):
            top = work.tile([P, P], F32, name="top")
            nc.vector.tensor_reduce(top[:], y_banks[n][:].rearrange("p d i -> p i d"), AX.X, ALU.max)
            tops[n] = top

        def exponentials(n):
            if n == last:
                z = inv3[:, :, :P]
            else:
                z_tile = work.tile([P, D, P], F32, name="z_tile")
                z = z_tile[:]
            nc.vector.tensor_tensor(z, y_banks[n][:], tops[n][:].unsqueeze(1).to_broadcast([P, D, P]), ALU.subtract)
            nc.scalar.activation(terms[n][:, E], z, ACT.Exp)

        def add_up(dst, src):
            count = src.shape[1]
            for d in range(count):
                nc.tensor.matmul(
                    dst, lhsT=src[:, d, :], rhs=ident[:], start=d == 0, stop=d == count - 1, is_transpose=True
                )

        def sum_shares(n):
            t, b = order[n]
            if b == 0:
                sum_e[t] = ps.tile([P, V], F32, name="sum_e")
                sum_rest[t] = ps.tile([P, 2, V], F32, name="sum_rest")
            cols = slice(b * P, (b + 1) * P)
            e, ee = terms[n][:, E], terms[n][:, EE]
            add_up(sum_e[t][:, cols], e)
            if n < SCALAR_SQUARES:
                nc.scalar.activation(ee, e, ACT.Square)
                add_up(sum_rest[t][:, 0, cols], ee)

        def sum_weighted(n):
            t, b = order[n]
            nc.vector.tensor_tensor(terms[n][:, EY], y_banks[n][:], terms[n][:, E], ALU.mult)
            if n + Y_BANKS <= last:
                scores(n + Y_BANKS)
            add_up(sum_rest[t][:, 1, b * P : (b + 1) * P], terms[n][:, EY])

        def sixth_power(t):
            second = work.tile([P, V], F32, name="second")
            third = work.tile([P, V], F32, name="third")
            nc.scalar.activation(second[:], sum_e[t][:], ACT.Square)
            nc.vector.tensor_tensor(third[:], sum_e[t][:], second[:], ALU.mult)
            nc.scalar.activation(sixth[t][:], third[:], ACT.Square)

        def numerator(t):
            scaled = work.tile([P, V], F32, name="scaled")
            nc.scalar.activation(scaled[:], sum_rest[t][:, 0, :], ACT.Copy, scale=unit_sb[:, t : t + 1])
            nc.vector.tensor_tensor(windows[t][:, V:], sum_rest[t][:, 1, :], scaled[:], ALU.mult)

        def finish(t):
            nc.scalar.activation(inv3[:, t, :], sixth[t][:], ACT.Abs_reciprocal_sqrt)
            if t < EARLY_PLANES:
                nc.vector.tensor_tensor(windows[t][:, :V], windows[t][:, V:], inv3[:, t, :], ALU.mult)
            else:
                nc.vector.tensor_tensor(windows[t][:, V:], sum_rest[t][:, 0, :], inv3[:, t, :], ALU.mult)
                nc.vector.scalar_tensor_tensor(
                    windows[t][:, :V], sum_rest[t][:, 1, :], unit_sb[:, t : t + 1], windows[t][:, V:], ALU.mult, ALU.mult
                )

        for n in range(Y_BANKS):
            scores(n)
        largest(0)
        for n in range(len(order)):
            t, b = order[n]
            if n < last:
                largest(n + 1)
            exponentials(n)
            if 0 < n <= Y_BANKS:
                sum_weighted(n - 1)
            sum_shares(n)
            if b == VB - 1:
                sixth_power(t)
            elif 0 < t <= EARLY_PLANES:
                numerator(t - 1)
        for n in range(Y_BANKS, len(order)):
            sum_weighted(n)
            if n >= SCALAR_SQUARES:
                nc.vector.tensor_tensor(terms[n][:, EE], terms[n][:, E], terms[n][:, E], ALU.mult)
        for n in range(SCALAR_SQUARES, len(order)):
            t, b = order[n]
            add_up(sum_rest[t][:, 0, b * P : (b + 1) * P], terms[n][:, EE])
        nc.vector.quantize_mx(w_codes[:].bitcast(FP8X4), w_sc[:], w_bf[:].rearrange("p n j -> p (n j)"))
        for t in range(PACK):
            finish(t)

        hid_planes = [keep.tile([P, PACK, HALF], BF16, name="hid_planes%d" % r) for r in range(2)]

        def fetch(t, r):
            cols = HALF // 16
            src = windows[t][:].indirect(use_sb[:, r * cols : (r + 1) * cols])
            if t == 0:
                nc.vector.tensor_copy(hid_planes[r][:, t, :], src)
            else:
                nc.scalar.activation(hid_planes[r][:, t, :], src, ACT.Copy)

        for r in range(2):
            for t in range(PACK):
                fetch(t, r)

        for r in range(2):
            hid_bf = keep.tile([P, HALF, PACK], BF16, name="hid_bf%d" % r, align_bytes=64)
            hid_codes = keep.tile([P, HALF], U32, name="hid_codes%d" % r, align_bytes=64)
            hid_sc = keep.tile([P, HALF], U8, name="hid_sc%d" % r, align_bytes=64)
            nc.vector.tensor_copy(
                hid_bf[:].rearrange("p (c i) t -> p c t i", i=4), hid_planes[r][:].rearrange("p t (c i) -> p c t i", i=4)
            )
            nc.vector.quantize_mx(hid_codes[:].bitcast(FP8X4), hid_sc[:], hid_bf[:].rearrange("p r t -> p (r t)"))
            for mt in range(N // P):
                acc = py.tile([P, D, P], F32, name="y")
                acc_cols = acc[:].rearrange("p d i -> p (d i)")[:, :HALF]
                nc.tensor.matmul_mx(
                    acc_cols,
                    lhsT=w_codes[:, mt * P : (mt + 1) * P].bitcast(FP8X4),
                    lhsT_scale=w_sc[:, mt * P : (mt + 1) * P],
                    rhs=hid_codes[:].bitcast(FP8X4),
                    rhs_scale=hid_sc[:],
                    start=True,
                    stop=True,
                )
                res = keep.tile([P, HALF], F32, name="res%d_%d" % (r, mt))
                if r == 1 and mt == 1:
                    nc.vector.tensor_copy(res[:], acc_cols)
                else:
                    nc.scalar.copy(res[:], acc_cols)
                queue = nc.scalar if r == 1 and mt == 0 else nc.sync
                queue.dma_start(out[mt * P : (mt + 1) * P, r * HALF : (r + 1) * HALF], res[:])
